import numpy as np
import ml_dtypes


def mxq(x, axis, fmt="e4m3"):
    dtype, down = {"e4m3": (ml_dtypes.float8_e4m3fn, 7), "e5m2": (ml_dtypes.float8_e5m2, 14)}[fmt]
    v = np.moveaxis(np.asarray(x, np.float32).astype(ml_dtypes.bfloat16).astype(np.float64), axis, -1)
    blocks = v.reshape(v.shape[:-1] + (-1, 32))
    amax = np.abs(blocks).max(-1, keepdims=True)
    byte = np.maximum(np.where(amax > 0, np.frexp(amax)[1] - 1 + 127, 0) - down, 1)
    scale = np.exp2(byte - 127.0)
    codes = (blocks / scale).astype(np.float32).astype(dtype).astype(np.float64)
    return np.moveaxis((codes * scale).reshape(v.shape), -1, axis)


WIDE = False


def mx_kscale(k):
    if not WIDE:
        return np.ones(k)
    levels = np.array([10, -10, 5, -5, 0])
    if k % 512:
        return np.exp2(np.random.permutation(np.resize(levels, k // 32))).repeat(32)
    a = np.empty((k // 512, 16))
    for p in range(k // 512):
        a[p, :8] = np.random.permutation(np.resize(levels, 8))
        for g in range(8):
            far = levels[np.abs(levels - a[p, g]) >= 10]
            a[p, g + 8] = far[np.random.randint(len(far))]
    return np.exp2(a.ravel()).repeat(32)


def f64(x):
    return np.asarray(x).astype(np.float64)


def striped(idx):
    return np.tile(np.asarray(idx).reshape(-1, 16).T, (8, 1)).astype(np.uint16)


def unstriped(offs):
    return offs[:16].T.reshape(-1).astype(np.int64)


B, N, T, D, DV, NQ = 2, 512, 2048, 512, 256, 128
PAGE = 16


def setup_inputs():
    n = np.random.standard_normal
    pages = np.random.permutation(T // PAGE)[:B * N // PAGE]
    idx = (pages[:, None] * PAGE + np.arange(PAGE)[None, :]).reshape(-1)
    s = mx_kscale(D)[:, None]
    u = np.ones(T)
    u[idx] = mx_kscale(B * N)
    r = np.random.uniform(0.5, 2.0, T)
    k = n((D, T)) / s
    v = n((DV, T)) / (u * r)
    return {
        "qT": (n((B, D, NQ)) * s * (0.60 / np.sqrt(D))).astype(np.float32),
        "kT": k.astype(np.float32),
        "vT": v.astype(np.float32),
        "vs": np.tile(u * r, (128, 1)).astype(np.float32),
        "sink": (2.0 + 3.0 * n((B, NQ, 1))).astype(np.float32),
        "offs": striped(idx),
    }


def reference(qT, kT, vT, vs, sink, offs):
    idx = unstriped(offs)
    k = f64(kT)
    v = f64(vT)
    pick = lambda x: x[:, idx].reshape(x.shape[0], B, N).transpose(1, 0, 2)
    q = f64(qT)
    score = mxq(q, 1, "e4m3").transpose(0, 2, 1) @ mxq(pick(k), 1, "e4m3")
    m = np.maximum(score.max(-1, keepdims=True), f64(sink))
    p = np.exp(score - m)
    total = p.sum(-1, keepdims=True) + np.exp(f64(sink) - m)
    w = p * pick(f64(vs))[:, :1, :]
    y = mxq(w, 2, "e4m3") @ mxq(pick(v).transpose(0, 2, 1), 1, "e4m3")
    y = y / total
    return y

@@ -1,0 +1,187 @@
+from contextlib import ExitStack
+
+import concourse.mybir as mybir
+from concourse.masks import make_identity
+
+B, N, T, D, DV, NQ = 2, 512, 2048, 512, 256, 128
+P = 128
+PACK = 4
+NV = DV // P
+
+FLOPS = 2 * B * N * NQ * (D + DV)
+BYTES = 4 * (B * D * NQ + D * T + DV * T + T + B * NQ + B * NQ * DV) + 2 * P * (B * N // 16)
+
+F32 = mybir.dt.float32
+BF16 = mybir.dt.bfloat16
+U32 = mybir.dt.uint32
+U16 = mybir.dt.uint16
+U8 = mybir.dt.uint8
+FP8X4 = mybir.dt.float8_e4m3fn_x4
+ACT = mybir.ActivationFunctionType
+ALU = mybir.AluOpType
+AX = mybir.AxisListType
+
+
+def tile_attend_sink_kernel(tc, qT, kT, vT, vs, sink, offs, out):
+    nc = tc.nc
+    with ExitStack() as ctx:
+        keep = ctx.enter_context(tc.tile_pool(name="keep", bufs=1))
+        banks = ctx.enter_context(tc.psum_pool(name="banks", bufs=1))
+
+        offsets = keep.tile([P, B * N // 16], U16, name="offsets")
+        scale_pool = keep.tile([P, T], F32, name="scale_pool")
+        warm = keep.tile([P, 1], F32, name="warm")
+        warmed = keep.tile([P, 1], F32, name="warmed")
+        ident = keep.tile([P, P], F32, name="ident")
+
+        nc.sync.dma_start(offsets[:], offs)
+        half = T // 2
+        nc.vector.memset(scale_pool[:, :half], 0.0)
+        nc.gpsimd.memset(scale_pool[:, half:], 0.0)
+        nc.vector.memset(warm[:], 0.0)
+        nc.scalar.activation(warmed[:], warm[:], ACT.Exp)
+        nc.scalar.dma_start(scale_pool[0:1, :], vs[0:1, :])
+        sinks = []
+        for b in range(B):
+            s = keep.tile([P, 1], F32, name="sink%d" % b)
+            nc.scalar.dma_start(s[:], sink[b])
+            sinks.append(s)
+
+        k_rows = kT.rearrange("(p t) c -> p t c", t=PACK)
+        k_pool = []
+        for t in range(PACK):
+            w = keep.tile([P, T], F32, name="k_pool%d" % t)
+            nc.sync.dma_start(w[:], k_rows[:, t, :])
+            k_pool.append(w)
+            if t == 0:
+                q_raw = keep.tile([P, B, PACK, NQ], F32, name="q_raw")
+                nc.sync.dma_start(q_raw[:], qT.rearrange("b (p t) q -> p b t q", t=PACK))
+        v_pool = []
+        for c in range(NV):
+            w = keep.tile([P, T], F32, name="v_pool%d" % c)
+            nc.sync.dma_start(w[:], vT[c * P : (c + 1) * P, :])
+            v_pool.append(w)
+
+        make_identity(nc, ident[:])
+
+        scale_row = keep.tile([P, B * N], F32, name="scale_row")
+        nc.vector.tensor_copy(scale_row[:], scale_pool[:].indirect(offsets[:]))
+        scale_col = keep.tile([P, B, PACK], F32, name="scale_col")
+        for b in range(B):
+            turned = banks.tile([P, PACK, P], F32, name="turned", tag="turned", bufs=4)
+            for t in range(PACK):
+                nc.tensor.transpose(turned[:, t, :], scale_row[:, b * N + t : (b + 1) * N : PACK], ident[:])
+            nc.scalar.copy(scale_col[:, b, :], turned[:, :, 0])
+
+        q_bf = keep.tile([P, B, NQ, PACK], BF16, name="q_bf", align_bytes=64)
+        for b in range(B):
+            nc.scalar.copy(q_bf[:, b], q_raw[:, b].rearrange("p t q -> p q t"))
+        q_codes = keep.tile([P, B * NQ], U32, name="q_codes", align_bytes=64)
+        q_scales = keep.tile([P, B * NQ], U8, name="q_scales", align_bytes=64)
+        nc.vector.quantize_mx(q_codes[:].bitcast(FP8X4), q_scales[:], q_bf[:].rearrange("p b q t -> p (b q t)"))
+
+        k_bf = []
+        for b in range(B):
+            k = keep.tile([P, N, PACK], BF16, name="k_bf%d" % b, align_bytes=64)
+            k_bf.append(k)
+        k_pair = keep.tile([P, 2, B * N], F32, name="k_pair")
+        for t in range(2):
+            nc.vector.tensor_copy(k_pair[:, t, :], k_pool[t][:].indirect(offsets[:]))
+        for b in range(B):
+            nc.scalar.copy(k_bf[b][:, :, 0:2], k_pair[:, :, b * N : (b + 1) * N].rearrange("p t n -> p n t"))
+        for t in (2, 3):
+            for b in range(B):
+                nc.vector.tensor_copy(k_bf[b][:, :, t], k_pool[t][:].indirect(offsets[:, b * N // 16 : (b + 1) * N // 16]))
+
+        probs = []
+        totals = []
+        for b in range(B):
+            k_codes = keep.tile([P, N], U32, name="k_codes%d" % b, align_bytes=64)
+            k_scales = keep.tile([P, N], U8, name="k_scales%d" % b, align_bytes=64)
+            nc.vector.quantize_mx(k_codes[:].bitcast(FP8X4), k_scales[:], k_bf[b][:].rearrange("p n t -> p (n t)"))
+            score = banks.tile([NQ, N], F32, name="score", tag="score", bufs=2)
+            nc.tensor.matmul_mx(
+                out=score[:],
+                lhsT=q_codes[:, b * NQ : (b + 1) * NQ].bitcast(FP8X4),
+                lhsT_scale=q_scales[:, b * NQ : (b + 1) * NQ],
+                rhs=k_codes[:].bitcast(FP8X4),
+                rhs_scale=k_scales[:],
+                start=True,
+                stop=True,
+            )
+            top = keep.tile([NQ, 1], F32, name="top%d" % b)
+            nc.vector.tensor_reduce(top[:], score[:], AX.X, ALU.max)
+            shift = keep.tile([NQ, 1], F32, name="shift%d" % b)
+            nc.vector.tensor_scalar(shift[:], top[:], sinks[b][:], -1.0, ALU.max, ALU.mult)
+            prob = keep.tile([NQ, PACK, P], F32, name="prob%d" % b)
+            listed = keep.tile([NQ, 1], F32, name="listed%d" % b)
+            nc.scalar.activation(
+                prob[:].rearrange("q t p -> q p t"),
+                score[:].rearrange("q (p t) -> q p t", t=PACK),
+                ACT.Exp,
+                bias=shift[:],
+                accum_out=listed[:],
+            )
+            probs.append(prob)
+            sunk = keep.tile([NQ, 1], F32, name="sunk%d" % b)
+            nc.scalar.activation(sunk[:], sinks[b][:], ACT.Exp, bias=shift[:])
+            totals.append((listed, sunk))
+
+        w_codes = []
+        for b in range(B):
+            turned = banks.tile([P, PACK, P], F32, name="turned", tag="turned", bufs=4)
+            for t in range(PACK):
+                nc.tensor.transpose(turned[:, t, :], probs[b][:, t, :], ident[:])
+            w_bf = keep.tile([P, NQ, PACK], BF16, name="w_bf%d" % b, align_bytes=64)
+            nc.vector.tensor_tensor(
+                w_bf[:],
+                turned[:].rearrange("p t q -> p q t"),
+                scale_col[:, b, :].unsqueeze(1).to_broadcast([P, NQ, PACK]),
+                ALU.mult,
+            )
+            codes = keep.tile([P, NQ], U32, name="w_codes%d" % b, align_bytes=64)
+            scales = keep.tile([P, NQ], U8, name="w_scales%d" % b, align_bytes=64)
+            nc.vector.quantize_mx(codes[:].bitcast(FP8X4), scales[:], w_bf[:].rearrange("p q t -> p (q t)"))
+            w_codes.append((codes, scales))
+
+        inverses = []
+        for b in range(B):
+            total = keep.tile([NQ, 1], F32, name="total%d" % b)
+            nc.gpsimd.tensor_tensor(total[:], totals[b][0][:], totals[b][1][:], ALU.add)
+            inverse = keep.tile([NQ, 1], F32, name="inverse%d" % b)
+            nc.vector.reciprocal(inverse[:], total[:])
+            inverses.append(inverse)
+
+        v_codes = {}
+        for c in range(NV):
+            v_row = keep.tile([P, B * N], F32, name="v_row%d" % c)
+            if c < NV - 1:
+                nc.vector.tensor_copy(v_row[:], v_pool[c][:].indirect(offsets[:]))
+            for b in range(B):
+                if c == NV - 1:
+                    nc.vector.tensor_copy(v_row[:, b * N : (b + 1) * N], v_pool[c][:].indirect(offsets[:, b * N // 16 : (b + 1) * N // 16]))
+                turned = banks.tile([P, PACK, P], F32, name="turned", tag="turned", bufs=4)
+                for t in range(PACK):
+                    nc.tensor.transpose(turned[:, t, :], v_row[:, b * N + t : (b + 1) * N : PACK], ident[:])
+                v_bf = keep.tile([P, P, PACK], BF16, name="v_bf%d%d" % (c, b), align_bytes=64)
+                nc.scalar.copy(v_bf[:], turned[:].rearrange("p t e -> p e t"))
+                codes = keep.tile([P, P], U32, name="v_codes%d%d" % (c, b), align_bytes=64)
+                scales = keep.tile([P, P], U8, name="v_scales%d%d" % (c, b), align_bytes=64)
+                nc.vector.quantize_mx(codes[:].bitcast(FP8X4), scales[:], v_bf[:].rearrange("p e t -> p (e t)"))
+                v_codes[(c, b)] = (codes, scales)
+
+        for b in range(B):
+            y = banks.tile([NQ, DV], F32, name="y", tag="y", bufs=2)
+            for c in range(NV):
+                nc.tensor.matmul_mx(
+                    out=y[:, c * P : (c + 1) * P],
+                    lhsT=w_codes[b][0][:].bitcast(FP8X4),
+                    lhsT_scale=w_codes[b][1][:],
+                    rhs=v_codes[(c, b)][0][:].bitcast(FP8X4),
+                    rhs_scale=v_codes[(c, b)][1][:],
+                    start=True,
+                    stop=True,
+                )
+            result = keep.tile([NQ, DV], F32, name="result%d" % b)
+            nc.scalar.activation(result[:], y[:], ACT.Copy, scale=inverses[b][:])
+            nc.sync.dma_start(out[b], result[:])

@@ -29,19 +29,25 @@ def tile_attend_sink_kernel(tc, qT, kT, vT, vs, sink, offs, out):
         banks = ctx.enter_context(tc.psum_pool(name="banks", bufs=1))
 
         offsets = keep.tile([P, B * N // 16], U16, name="offsets")
+
+        def listed(b):
+            return offsets[:, b * N // 16 : (b + 1) * N // 16]
+
         scale_pool = keep.tile([P, T], F32, name="scale_pool")
         warm = keep.tile([P, 1], F32, name="warm")
         warmed = keep.tile([P, 1], F32, name="warmed")
         ident = keep.tile([P, P], F32, name="ident")
+        ident_bf = keep.tile([P, P], BF16, name="ident_bf")
 
         nc.sync.dma_start(offsets[:], offs)
         half = T // 2
         nc.vector.memset(scale_pool[:, :half], 0.0)
         nc.gpsimd.memset(scale_pool[:, half:], 0.0)
-        nc.vector.memset(warm[:], 0.0)
-        nc.scalar.activation(warmed[:], warm[:], ACT.Exp)
         nc.scalar.dma_start(scale_pool[0:1, :], vs[0:1, :])
+        nc.gpsimd.memset(warm[:], 0.0)
+        nc.scalar.activation(warmed[:], warm[:], ACT.Exp)
         sinks = []
+        neg_sinks = []
         for b in range(B):
             s = keep.tile([P, 1], F32, name="sink%d" % b)
             nc.scalar.dma_start(s[:], sink[b])
@@ -53,9 +59,11 @@ def tile_attend_sink_kernel(tc, qT, kT, vT, vs, sink, offs, out):
             w = keep.tile([P, T], F32, name="k_pool%d" % t)
             nc.sync.dma_start(w[:], k_rows[:, t, :])
             k_pool.append(w)
-            if t == 0:
-                q_raw = keep.tile([P, B, PACK, NQ], F32, name="q_raw")
-                nc.sync.dma_start(q_raw[:], qT.rearrange("b (p t) q -> p b t q", t=PACK))
+        q_raw = []
+        for b in range(B):
+            q = keep.tile([P, PACK, NQ], F32, name="q_raw%d" % b)
+            nc.sync.dma_start(q[:], qT[b].rearrange("(p t) q -> p t q", t=PACK))
+            q_raw.append(q)
         v_pool = []
         for c in range(NV):
             w = keep.tile([P, T], F32, name="v_pool%d" % c)
@@ -63,73 +71,103 @@ def tile_attend_sink_kernel(tc, qT, kT, vT, vs, sink, offs, out):
             v_pool.append(w)
 
         make_identity(nc, ident[:])
+        make_identity(nc, ident_bf[:])
+        for b in range(B):
+            s = keep.tile([P, 1], F32, name="neg_sink%d" % b)
+            nc.gpsimd.tensor_scalar(s[:], sinks[b][:], -1.0, None, ALU.mult)
+            neg_sinks.append(s)
 
         scale_row = keep.tile([P, B * N], F32, name="scale_row")
         nc.vector.tensor_copy(scale_row[:], scale_pool[:].indirect(offsets[:]))
         scale_col = keep.tile([P, B, PACK], F32, name="scale_col")
         for b in range(B):
-            turned = banks.tile([P, PACK, P], F32, name="turned", tag="turned", bufs=4)
+            turned = banks.tile([P, PACK, P], F32, name="turned", tag="turned", bufs=2)
             for t in range(PACK):
                 nc.tensor.transpose(turned[:, t, :], scale_row[:, b * N + t : (b + 1) * N : PACK], ident[:])
             nc.scalar.copy(scale_col[:, b, :], turned[:, :, 0])
-
-        q_bf = keep.tile([P, B, NQ, PACK], BF16, name="q_bf", align_bytes=64)
-        for b in range(B):
-            nc.scalar.copy(q_bf[:, b], q_raw[:, b].rearrange("p t q -> p q t"))
-        q_codes = keep.tile([P, B * NQ], U32, name="q_codes", align_bytes=64)
-        q_scales = keep.tile([P, B * NQ], U8, name="q_scales", align_bytes=64)
-        nc.vector.quantize_mx(q_codes[:].bitcast(FP8X4), q_scales[:], q_bf[:].rearrange("p b q t -> p (b q t)"))
 
         k_bf = []
         for b in range(B):
             k = keep.tile([P, N, PACK], BF16, name="k_bf%d" % b, align_bytes=64)
             k_bf.append(k)
-        k_pair = keep.tile([P, 2, B * N], F32, name="k_pair")
+        k_low = keep.tile([P, 2, B * N], F32, name="k_low")
+        k_high = keep.tile([P, 2, B * N], F32, name="k_high")
         for t in range(2):
-            nc.vector.tensor_copy(k_pair[:, t, :], k_pool[t][:].indirect(offsets[:]))
+            nc.vector.tensor_copy(k_low[:, t, :], k_pool[t][:].indirect(offsets[:]))
         for b in range(B):
-            nc.scalar.copy(k_bf[b][:, :, 0:2], k_pair[:, :, b * N : (b + 1) * N].rearrange("p t n -> p n t"))
-        for t in (2, 3):
-            for b in range(B):
-                nc.vector.tensor_copy(k_bf[b][:, :, t], k_pool[t][:].indirect(offsets[:, b * N // 16 : (b + 1) * N // 16]))
+            nc.scalar.copy(k_bf[b][:, :, 0:2], k_low[:, :, b * N : (b + 1) * N].rearrange("p t n -> p n t"))
+        nc.vector.tensor_copy(k_high[:, 0, :], k_pool[2][:].indirect(offsets[:]))
 
-        probs = []
-        totals = []
+        q_codes = []
         for b in range(B):
-            k_codes = keep.tile([P, N], U32, name="k_codes%d" % b, align_bytes=64)
-            k_scales = keep.tile([P, N], U8, name="k_scales%d" % b, align_bytes=64)
-            nc.vector.quantize_mx(k_codes[:].bitcast(FP8X4), k_scales[:], k_bf[b][:].rearrange("p n t -> p (n t)"))
+            q_bf = keep.tile([P, NQ, PACK], BF16, name="q_bf%d" % b, align_bytes=64)
+            nc.scalar.copy(q_bf[:], q_raw[b][:].rearrange("p t q -> p q t"))
+            codes = keep.tile([P, NQ], U32, name="q_codes%d" % b, align_bytes=64)
+            scales = keep.tile([P, NQ], U8, name="q_scales%d" % b, align_bytes=64)
+            nc.vector.quantize_mx(codes[:].bitcast(FP8X4), scales[:], q_bf[:].rearrange("p q t -> p (q t)"))
+            q_codes.append((codes, scales))
+
+        for b in range(B):
+            nc.vector.tensor_copy(k_high[:, 1, b * N : (b + 1) * N], k_pool[3][:].indirect(listed(b)))
+        scores = []
+        for b in range(B):
+            copy = nc.vector.tensor_copy if b == 0 else nc.scalar.copy
+            copy(k_bf[b][:, :, 2:4], k_high[:, :, b * N : (b + 1) * N].rearrange("p t n -> p n t"))
+            codes = keep.tile([P, N], U32, name="k_codes%d" % b, align_bytes=64)
+            scales = keep.tile([P, N], U8, name="k_scales%d" % b, align_bytes=64)
+            nc.vector.quantize_mx(codes[:].bitcast(FP8X4), scales[:], k_bf[b][:].rearrange("p n t -> p (n t)"))
             score = banks.tile([NQ, N], F32, name="score", tag="score", bufs=2)
             nc.tensor.matmul_mx(
                 out=score[:],
-                lhsT=q_codes[:, b * NQ : (b + 1) * NQ].bitcast(FP8X4),
-                lhsT_scale=q_scales[:, b * NQ : (b + 1) * NQ],
-                rhs=k_codes[:].bitcast(FP8X4),
-                rhs_scale=k_scales[:],
+                lhsT=q_codes[b][0][:].bitcast(FP8X4),
+                lhsT_scale=q_codes[b][1][:],
+                rhs=codes[:].bitcast(FP8X4),
+                rhs_scale=scales[:],
                 start=True,
                 stop=True,
             )
-            top = keep.tile([NQ, 1], F32, name="top%d" % b)
-            nc.vector.tensor_reduce(top[:], score[:], AX.X, ALU.max)
+            scores.append(score)
+
+        probs = []
+        totals = []
+        shifts = []
+        for b in range(B):
+            junk = keep.tile([NQ, N], F32, name="junk%d" % b)
             shift = keep.tile([NQ, 1], F32, name="shift%d" % b)
-            nc.vector.tensor_scalar(shift[:], top[:], sinks[b][:], -1.0, ALU.max, ALU.mult)
+            nc.vector.tensor_scalar(junk[:], scores[b][:], -1.0, neg_sinks[b][:], ALU.mult, ALU.min, accum_out=shift[:])
             prob = keep.tile([NQ, PACK, P], F32, name="prob%d" % b)
-            listed = keep.tile([NQ, 1], F32, name="listed%d" % b)
+            total = keep.tile([NQ, 1], F32, name="listed%d" % b)
             nc.scalar.activation(
                 prob[:].rearrange("q t p -> q p t"),
-                score[:].rearrange("q (p t) -> q p t", t=PACK),
+                scores[b][:].rearrange("q (p t) -> q p t", t=PACK),
                 ACT.Exp,
                 bias=shift[:],
-                accum_out=listed[:],
+                accum_out=total[:],
             )
             probs.append(prob)
+            totals.append(total)
+            shifts.append(shift)
+        sunks = []
+        for b in range(B):
             sunk = keep.tile([NQ, 1], F32, name="sunk%d" % b)
-            nc.scalar.activation(sunk[:], sinks[b][:], ACT.Exp, bias=shift[:])
-            totals.append((listed, sunk))
+            nc.scalar.activation(sunk[:], sinks[b][:], ACT.Exp, bias=shifts[b][:])
+            sunks.append(sunk)
+
+        v_bfs = {}
+        for c in range(NV):
+            for b in range(B):
+                v_row = keep.tile([P, PACK, P], BF16, name="v_row%d%d" % (c, b))
+                nc.vector.tensor_copy(v_row[:].rearrange("e t p -> e p t"), v_pool[c][:].indirect(listed(b)))
+                turned_v = banks.tile([P, PACK, P], BF16, name="turned_v", tag="turned_v", bufs=2)
+                for t in range(PACK):
+                    nc.tensor.transpose(turned_v[:, t, :], v_row[:, t, :], ident_bf[:])
+                v_bf = keep.tile([P, P, PACK], BF16, name="v_bf%d%d" % (c, b), align_bytes=64)
+                nc.scalar.copy(v_bf[:], turned_v[:].rearrange("p t e -> p e t"))
+                v_bfs[(c, b)] = v_bf
 
         w_codes = []
         for b in range(B):
-            turned = banks.tile([P, PACK, P], F32, name="turned", tag="turned", bufs=4)
+            turned = banks.tile([P, PACK, P], F32, name="turned", tag="turned", bufs=2)
             for t in range(PACK):
                 nc.tensor.transpose(turned[:, t, :], probs[b][:, t, :], ident[:])
             w_bf = keep.tile([P, NQ, PACK], BF16, name="w_bf%d" % b, align_bytes=64)
@@ -147,27 +185,17 @@ def tile_attend_sink_kernel(tc, qT, kT, vT, vs, sink, offs, out):
         inverses = []
         for b in range(B):
             total = keep.tile([NQ, 1], F32, name="total%d" % b)
-            nc.gpsimd.tensor_tensor(total[:], totals[b][0][:], totals[b][1][:], ALU.add)
+            nc.gpsimd.tensor_tensor(total[:], totals[b][:], sunks[b][:], ALU.add)
             inverse = keep.tile([NQ, 1], F32, name="inverse%d" % b)
             nc.vector.reciprocal(inverse[:], total[:])
             inverses.append(inverse)
 
         v_codes = {}
         for c in range(NV):
-            v_row = keep.tile([P, B * N], F32, name="v_row%d" % c)
-            if c < NV - 1:
-                nc.vector.tensor_copy(v_row[:], v_pool[c][:].indirect(offsets[:]))
             for b in range(B):
-                if c == NV - 1:
-                    nc.vector.tensor_copy(v_row[:, b * N : (b + 1) * N], v_pool[c][:].indirect(offsets[:, b * N // 16 : (b + 1) * N // 16]))
-                turned = banks.tile([P, PACK, P], F32, name="turned", tag="turned", bufs=4)
-                for t in range(PACK):
-                    nc.tensor.transpose(turned[:, t, :], v_row[:, b * N + t : (b + 1) * N : PACK], ident[:])
-                v_bf = keep.tile([P, P, PACK], BF16, name="v_bf%d%d" % (c, b), align_bytes=64)
-                nc.scalar.copy(v_bf[:], turned[:].rearrange("p t e -> p e t"))
                 codes = keep.tile([P, P], U32, name="v_codes%d%d" % (c, b), align_bytes=64)
                 scales = keep.tile([P, P], U8, name="v_scales%d%d" % (c, b), align_bytes=64)
-                nc.vector.quantize_mx(codes[:].bitcast(FP8X4), scales[:], v_bf[:].rearrange("p e t -> p (e t)"))
+                nc.vector.quantize_mx(codes[:].bitcast(FP8X4), scales[:], v_bfs[(c, b)][:].rearrange("p e t -> p (e t)"))
                 v_codes[(c, b)] = (codes, scales)
 
         for b in range(B):

@@ -43,7 +43,6 @@ def tile_attend_sink_kernel(tc, qT, kT, vT, vs, sink, offs, out):
         half = T // 2
         nc.vector.memset(scale_pool[:, :half], 0.0)
         nc.gpsimd.memset(scale_pool[:, half:], 0.0)
-        nc.scalar.dma_start(scale_pool[0:1, :], vs[0:1, :])
         nc.gpsimd.memset(warm[:], 0.0)
         nc.scalar.activation(warmed[:], warm[:], ACT.Exp)
         sinks = []
@@ -59,6 +58,8 @@ def tile_attend_sink_kernel(tc, qT, kT, vT, vs, sink, offs, out):
             w = keep.tile([P, T], F32, name="k_pool%d" % t)
             nc.sync.dma_start(w[:], k_rows[:, t, :])
             k_pool.append(w)
+            if t == 1:
+                nc.sync.dma_start(scale_pool[0:1, :], vs[0:1, :])
         q_raw = []
         for b in range(B):
             q = keep.tile([P, PACK, NQ], F32, name="q_raw%d" % b)
@@ -77,6 +78,17 @@ def tile_attend_sink_kernel(tc, qT, kT, vT, vs, sink, offs, out):
             nc.gpsimd.tensor_scalar(s[:], sinks[b][:], -1.0, None, ALU.mult)
             neg_sinks.append(s)
 
+        k_bf = []
+        for b in range(B):
+            k = keep.tile([P, N, PACK], BF16, name="k_bf%d" % b, align_bytes=64)
+            k_bf.append(k)
+        k_low = keep.tile([P, 2, B * N], F32, name="k_low", tag="low", align_bytes=64)
+        k_high = keep.tile([P, 2, B * N], F32, name="k_high")
+        for t in range(2):
+            nc.vector.tensor_copy(k_low[:, t, :], k_pool[t][:].indirect(offsets[:]))
+        for b in range(B):
+            nc.scalar.copy(k_bf[b][:, :, 0:2], k_low[:, :, b * N : (b + 1) * N].rearrange("p t n -> p n t"))
+
         scale_row = keep.tile([P, B * N], F32, name="scale_row")
         nc.vector.tensor_copy(scale_row[:], scale_pool[:].indirect(offsets[:]))
         scale_col = keep.tile([P, B, PACK], F32, name="scale_col")
@@ -86,130 +98,124 @@ def tile_attend_sink_kernel(tc, qT, kT, vT, vs, sink, offs, out):
                 nc.tensor.transpose(turned[:, t, :], scale_row[:, b * N + t : (b + 1) * N : PACK], ident[:])
             nc.scalar.copy(scale_col[:, b, :], turned[:, :, 0])
 
-        k_bf = []
-        for b in range(B):
-            k = keep.tile([P, N, PACK], BF16, name="k_bf%d" % b, align_bytes=64)
-            k_bf.append(k)
-        k_low = keep.tile([P, 2, B * N], F32, name="k_low")
-        k_high = keep.tile([P, 2, B * N], F32, name="k_high")
-        for t in range(2):
-            nc.vector.tensor_copy(k_low[:, t, :], k_pool[t][:].indirect(offsets[:]))
-        for b in range(B):
-            nc.scalar.copy(k_bf[b][:, :, 0:2], k_low[:, :, b * N : (b + 1) * N].rearrange("p t n -> p n t"))
         nc.vector.tensor_copy(k_high[:, 0, :], k_pool[2][:].indirect(offsets[:]))
-
-        q_codes = []
-        for b in range(B):
-            q_bf = keep.tile([P, NQ, PACK], BF16, name="q_bf%d" % b, align_bytes=64)
-            nc.scalar.copy(q_bf[:], q_raw[b][:].rearrange("p t q -> p q t"))
-            codes = keep.tile([P, NQ], U32, name="q_codes%d" % b, align_bytes=64)
-            scales = keep.tile([P, NQ], U8, name="q_scales%d" % b, align_bytes=64)
-            nc.vector.quantize_mx(codes[:].bitcast(FP8X4), scales[:], q_bf[:].rearrange("p q t -> p (q t)"))
-            q_codes.append((codes, scales))
-
         for b in range(B):
             nc.vector.tensor_copy(k_high[:, 1, b * N : (b + 1) * N], k_pool[3][:].indirect(listed(b)))
-        scores = []
         for b in range(B):
             copy = nc.vector.tensor_copy if b == 0 else nc.scalar.copy
             copy(k_bf[b][:, :, 2:4], k_high[:, :, b * N : (b + 1) * N].rearrange("p t n -> p n t"))
-            codes = keep.tile([P, N], U32, name="k_codes%d" % b, align_bytes=64)
-            scales = keep.tile([P, N], U8, name="k_scales%d" % b, align_bytes=64)
-            nc.vector.quantize_mx(codes[:].bitcast(FP8X4), scales[:], k_bf[b][:].rearrange("p n t -> p (n t)"))
-            score = banks.tile([NQ, N], F32, name="score", tag="score", bufs=2)
+
+        q_bf = keep.tile([P, B, NQ, PACK], BF16, name="q_bf", tag="low", align_bytes=64)
+        for b in range(B):
+            nc.scalar.copy(q_bf[:, b], q_raw[b][:].rearrange("p t q -> p q t"))
+
+        q_codes = {}
+        k_codes = {}
+        w_codes = {}
+        v_codes = {}
+        v_bf = {}
+        scores = {}
+        probs = {}
+        shifts = {}
+        sums = {}
+
+        def quantize(store, key, tile_2d, width, name):
+            codes = keep.tile([P, width], U32, name=name + "_codes%d" % key, align_bytes=64)
+            scales = keep.tile([P, width], U8, name=name + "_scales%d" % key, align_bytes=64)
+            nc.vector.quantize_mx(codes[:].bitcast(FP8X4), scales[:], tile_2d)
+            store[key] = (codes, scales)
+
+        def multiply(bank, left, right):
             nc.tensor.matmul_mx(
-                out=score[:],
-                lhsT=q_codes[b][0][:].bitcast(FP8X4),
-                lhsT_scale=q_codes[b][1][:],
-                rhs=codes[:].bitcast(FP8X4),
-                rhs_scale=scales[:],
+                out=bank,
+                lhsT=left[0][:].bitcast(FP8X4),
+                lhsT_scale=left[1][:],
+                rhs=right[0][:].bitcast(FP8X4),
+                rhs_scale=right[1][:],
                 start=True,
                 stop=True,
             )
-            scores.append(score)
 
-        probs = []
-        totals = []
-        shifts = []
-        for b in range(B):
+        def score(b):
+            quantize(q_codes, b, q_bf[:, b].rearrange("p q t -> p (q t)"), NQ, "q")
+            quantize(k_codes, b, k_bf[b][:].rearrange("p n t -> p (n t)"), N, "k")
+            bank = banks.tile([NQ, N], F32, name="score", tag="score", bufs=2)
+            multiply(bank[:], q_codes[b], k_codes[b])
+            scores[b] = bank
+
+        def weigh(b):
             junk = keep.tile([NQ, N], F32, name="junk%d" % b)
             shift = keep.tile([NQ, 1], F32, name="shift%d" % b)
             nc.vector.tensor_scalar(junk[:], scores[b][:], -1.0, neg_sinks[b][:], ALU.mult, ALU.min, accum_out=shift[:])
             prob = keep.tile([NQ, PACK, P], F32, name="prob%d" % b)
-            total = keep.tile([NQ, 1], F32, name="listed%d" % b)
+            own = keep.tile([NQ, 1], F32, name="own%d" % b)
             nc.scalar.activation(
                 prob[:].rearrange("q t p -> q p t"),
                 scores[b][:].rearrange("q (p t) -> q p t", t=PACK),
                 ACT.Exp,
                 bias=shift[:],
-                accum_out=total[:],
+                accum_out=own[:],
             )
-            probs.append(prob)
-            totals.append(total)
-            shifts.append(shift)
-        sunks = []
+            probs[b] = prob
+            shifts[b] = shift
+            sums[b] = own
+
         for b in range(B):
-            sunk = keep.tile([NQ, 1], F32, name="sunk%d" % b)
-            nc.scalar.activation(sunk[:], sinks[b][:], ACT.Exp, bias=shifts[b][:])
-            sunks.append(sunk)
+            v = keep.tile([P, NV, P, PACK], BF16, name="v_bf%d" % b, align_bytes=64)
+            v_bf[b] = v
 
-        v_bfs = {}
-        for c in range(NV):
-            for b in range(B):
-                v_row = keep.tile([P, PACK, P], BF16, name="v_row%d%d" % (c, b))
-                nc.vector.tensor_copy(v_row[:].rearrange("e t p -> e p t"), v_pool[c][:].indirect(listed(b)))
-                turned_v = banks.tile([P, PACK, P], BF16, name="turned_v", tag="turned_v", bufs=2)
-                for t in range(PACK):
-                    nc.tensor.transpose(turned_v[:, t, :], v_row[:, t, :], ident_bf[:])
-                v_bf = keep.tile([P, P, PACK], BF16, name="v_bf%d%d" % (c, b), align_bytes=64)
-                nc.scalar.copy(v_bf[:], turned_v[:].rearrange("p t e -> p e t"))
-                v_bfs[(c, b)] = v_bf
+        def turn_values(c, b):
+            v_row = keep.tile([P, PACK, P], BF16, name="v_row%d%d" % (c, b))
+            nc.vector.tensor_copy(v_row[:].rearrange("e t p -> e p t"), v_pool[c][:].indirect(listed(b)))
+            turned_v = banks.tile([P, PACK, P], BF16, name="turned_v", tag="turned_v", bufs=2)
+            for t in range(PACK):
+                nc.tensor.transpose(turned_v[:, t, :], v_row[:, t, :], ident_bf[:])
+            nc.scalar.copy(v_bf[b][:, c], turned_v[:].rearrange("p t e -> p e t"))
 
-        w_codes = []
+        score(0)
+        turn_values(0, 0)
+        score(1)
+        weigh(0)
+        turn_values(1, 0)
+        weigh(1)
+        turn_values(0, 1)
+        turn_values(1, 1)
+
+        sunk = []
+        for b in range(B):
+            s = keep.tile([NQ, 1], F32, name="sunk%d" % b)
+            nc.scalar.activation(s[:], sinks[b][:], ACT.Exp, bias=shifts[b][:])
+            sunk.append(s)
+
+        w_bf = []
         for b in range(B):
             turned = banks.tile([P, PACK, P], F32, name="turned", tag="turned", bufs=2)
             for t in range(PACK):
                 nc.tensor.transpose(turned[:, t, :], probs[b][:, t, :], ident[:])
-            w_bf = keep.tile([P, NQ, PACK], BF16, name="w_bf%d" % b, align_bytes=64)
+            w = keep.tile([P, NQ, PACK], BF16, name="w_bf%d" % b, align_bytes=64)
             nc.vector.tensor_tensor(
-                w_bf[:],
+                w[:],
                 turned[:].rearrange("p t q -> p q t"),
                 scale_col[:, b, :].unsqueeze(1).to_broadcast([P, NQ, PACK]),
                 ALU.mult,
             )
-            codes = keep.tile([P, NQ], U32, name="w_codes%d" % b, align_bytes=64)
-            scales = keep.tile([P, NQ], U8, name="w_scales%d" % b, align_bytes=64)
-            nc.vector.quantize_mx(codes[:].bitcast(FP8X4), scales[:], w_bf[:].rearrange("p q t -> p (q t)"))
-            w_codes.append((codes, scales))
+            w_bf.append(w)
+        for b in range(B):
+            quantize(w_codes, b, w_bf[b][:].rearrange("p q t -> p (q t)"), NQ, "w")
+        for b in range(B):
+            quantize(v_codes, b, v_bf[b][:].rearrange("p c e t -> p (c e t)"), DV, "v")
 
         inverses = []
         for b in range(B):
             total = keep.tile([NQ, 1], F32, name="total%d" % b)
-            nc.gpsimd.tensor_tensor(total[:], totals[b][:], sunks[b][:], ALU.add)
+            nc.gpsimd.tensor_tensor(total[:], sums[b][:], sunk[b][:], ALU.add)
             inverse = keep.tile([NQ, 1], F32, name="inverse%d" % b)
             nc.vector.reciprocal(inverse[:], total[:])
             inverses.append(inverse)
 
-        v_codes = {}
-        for c in range(NV):
-            for b in range(B):
-                codes = keep.tile([P, P], U32, name="v_codes%d%d" % (c, b), align_bytes=64)
-                scales = keep.tile([P, P], U8, name="v_scales%d%d" % (c, b), align_bytes=64)
-                nc.vector.quantize_mx(codes[:].bitcast(FP8X4), scales[:], v_bfs[(c, b)][:].rearrange("p e t -> p (e t)"))
-                v_codes[(c, b)] = (codes, scales)
-
         for b in range(B):
             y = banks.tile([NQ, DV], F32, name="y", tag="y", bufs=2)
-            for c in range(NV):
-                nc.tensor.matmul_mx(
-                    out=y[:, c * P : (c + 1) * P],
-                    lhsT=w_codes[b][0][:].bitcast(FP8X4),
-                    lhsT_scale=w_codes[b][1][:],
-                    rhs=v_codes[(c, b)][0][:].bitcast(FP8X4),
-                    rhs_scale=v_codes[(c, b)][1][:],
-                    start=True,
-                    stop=True,
-                )
+            multiply(y[:], w_codes[b], v_codes[b])
             result = keep.tile([NQ, DV], F32, name="result%d" % b)
             nc.scalar.activation(result[:], y[:], ACT.Copy, scale=inverses[b][:])
             nc.sync.dma_start(out[b], result[:])

@@ -34,6 +34,7 @@ def tile_attend_sink_kernel(tc, qT, kT, vT, vs, sink, offs, out):
             return offsets[:, b * N // 16 : (b + 1) * N // 16]
 
         scale_pool = keep.tile([P, T], F32, name="scale_pool")
+        sink_rows = keep.tile([P, P], F32, name="sink_rows")
         warm = keep.tile([P, 1], F32, name="warm")
         warmed = keep.tile([P, 1], F32, name="warmed")
         ident = keep.tile([P, P], F32, name="ident")
@@ -43,14 +44,9 @@ def tile_attend_sink_kernel(tc, qT, kT, vT, vs, sink, offs, out):
         half = T // 2
         nc.vector.memset(scale_pool[:, :half], 0.0)
         nc.gpsimd.memset(scale_pool[:, half:], 0.0)
+        nc.gpsimd.memset(sink_rows[:], 0.0)
         nc.gpsimd.memset(warm[:], 0.0)
         nc.scalar.activation(warmed[:], warm[:], ACT.Exp)
-        sinks = []
-        neg_sinks = []
-        for b in range(B):
-            s = keep.tile([P, 1], F32, name="sink%d" % b)
-            nc.scalar.dma_start(s[:], sink[b])
-            sinks.append(s)
 
         k_rows = kT.rearrange("(p t) c -> p t c", t=PACK)
         k_pool = []
@@ -58,8 +54,9 @@ def tile_attend_sink_kernel(tc, qT, kT, vT, vs, sink, offs, out):
             w = keep.tile([P, T], F32, name="k_pool%d" % t)
             nc.sync.dma_start(w[:], k_rows[:, t, :])
             k_pool.append(w)
-            if t == 1:
+            if t == 0:
                 nc.sync.dma_start(scale_pool[0:1, :], vs[0:1, :])
+                nc.sync.dma_start(sink_rows[0:B, :], sink.rearrange("b q o -> b (q o)"))
         q_raw = []
         for b in range(B):
             q = keep.tile([P, PACK, NQ], F32, name="q_raw%d" % b)
@@ -73,10 +70,13 @@ def tile_attend_sink_kernel(tc, qT, kT, vT, vs, sink, offs, out):
 
         make_identity(nc, ident[:])
         make_identity(nc, ident_bf[:])
-        for b in range(B):
-            s = keep.tile([P, 1], F32, name="neg_sink%d" % b)
-            nc.gpsimd.tensor_scalar(s[:], sinks[b][:], -1.0, None, ALU.mult)
-            neg_sinks.append(s)
+
+        turned_sink = banks.tile([P, PACK, P], F32, name="turned_sink", tag="turned", bufs=2)
+        nc.tensor.transpose(turned_sink[:, 0, :], sink_rows[:], ident[:])
+        sink_col = keep.tile([NQ, B], F32, name="sink_col")
+        nc.scalar.copy(sink_col[:], turned_sink[:, 0, 0:B])
+        neg_sink = keep.tile([NQ, B], F32, name="neg_sink")
+        nc.gpsimd.tensor_scalar(neg_sink[:], sink_col[:], -1.0, None, ALU.mult)
 
         k_bf = []
         for b in range(B):
@@ -84,11 +84,11 @@ def tile_attend_sink_kernel(tc, qT, kT, vT, vs, sink, offs, out):
             k_bf.append(k)
         k_low = keep.tile([P, 2, B * N], F32, name="k_low", tag="low", align_bytes=64)
         k_high = keep.tile([P, 2, B * N], F32, name="k_high")
-        for t in range(2):
-            nc.vector.tensor_copy(k_low[:, t, :], k_pool[t][:].indirect(offsets[:]))
-        for b in range(B):
-            nc.scalar.copy(k_bf[b][:, :, 0:2], k_low[:, :, b * N : (b + 1) * N].rearrange("p t n -> p n t"))
 
+        def pair(copy, b, planes, t0):
+            copy(k_bf[b][:, :, t0 : t0 + 2], planes[:, :, b * N : (b + 1) * N].rearrange("p t n -> p n t"))
+
+        nc.vector.tensor_copy(k_low[:, 0, :], k_pool[0][:].indirect(offsets[:]))
         scale_row = keep.tile([P, B * N], F32, name="scale_row")
         nc.vector.tensor_copy(scale_row[:], scale_pool[:].indirect(offsets[:]))
         scale_col = keep.tile([P, B, PACK], F32, name="scale_col")
@@ -97,33 +97,24 @@ def tile_attend_sink_kernel(tc, qT, kT, vT, vs, sink, offs, out):
             for t in range(PACK):
                 nc.tensor.transpose(turned[:, t, :], scale_row[:, b * N + t : (b + 1) * N : PACK], ident[:])
             nc.scalar.copy(scale_col[:, b, :], turned[:, :, 0])
-
+        nc.vector.tensor_copy(k_low[:, 1, :], k_pool[1][:].indirect(offsets[:]))
         nc.vector.tensor_copy(k_high[:, 0, :], k_pool[2][:].indirect(offsets[:]))
+        pair(nc.scalar.copy, 0, k_low, 0)
+        pair(nc.vector.tensor_copy, 1, k_low, 0)
         for b in range(B):
             nc.vector.tensor_copy(k_high[:, 1, b * N : (b + 1) * N], k_pool[3][:].indirect(listed(b)))
-        for b in range(B):
-            copy = nc.vector.tensor_copy if b == 0 else nc.scalar.copy
-            copy(k_bf[b][:, :, 2:4], k_high[:, :, b * N : (b + 1) * N].rearrange("p t n -> p n t"))
+        pair(nc.vector.tensor_copy, 0, k_high, 2)
+        pair(nc.scalar.copy, 1, k_high, 2)
 
         q_bf = keep.tile([P, B, NQ, PACK], BF16, name="q_bf", tag="low", align_bytes=64)
         for b in range(B):
             nc.scalar.copy(q_bf[:, b], q_raw[b][:].rearrange("p t q -> p q t"))
 
-        q_codes = {}
-        k_codes = {}
-        w_codes = {}
-        v_codes = {}
-        v_bf = {}
-        scores = {}
-        probs = {}
-        shifts = {}
-        sums = {}
-
-        def quantize(store, key, tile_2d, width, name):
-            codes = keep.tile([P, width], U32, name=name + "_codes%d" % key, align_bytes=64)
-            scales = keep.tile([P, width], U8, name=name + "_scales%d" % key, align_bytes=64)
-            nc.vector.quantize_mx(codes[:].bitcast(FP8X4), scales[:], tile_2d)
-            store[key] = (codes, scales)
+        def quantize(name, source, width):
+            codes = keep.tile([P, width], U32, name=name + "_codes", align_bytes=64)
+            scales = keep.tile([P, width], U8, name=name + "_scales", align_bytes=64)
+            nc.vector.quantize_mx(codes[:].bitcast(FP8X4), scales[:], source)
+            return codes, scales
 
         def multiply(bank, left, right):
             nc.tensor.matmul_mx(
@@ -136,86 +127,91 @@ def tile_attend_sink_kernel(tc, qT, kT, vT, vs, sink, offs, out):
                 stop=True,
             )
 
-        def score(b):
-            quantize(q_codes, b, q_bf[:, b].rearrange("p q t -> p (q t)"), NQ, "q")
-            quantize(k_codes, b, k_bf[b][:].rearrange("p n t -> p (n t)"), N, "k")
-            bank = banks.tile([NQ, N], F32, name="score", tag="score", bufs=2)
-            multiply(bank[:], q_codes[b], k_codes[b])
-            scores[b] = bank
+        scores = {}
+        probs = {}
+        shifts = {}
+        v_bf = {}
+        w_bf = {}
+        w_mx = {}
+        v_mx = {}
+        own = keep.tile([NQ, B], F32, name="own")
+
+        def score(b, q_mx):
+            k_mx = quantize("k%d" % b, k_bf[b][:].rearrange("p n t -> p (n t)"), N)
+            scores[b] = banks.tile([NQ, N], F32, name="score", tag="score", bufs=2)
+            multiply(scores[b][:], q_mx, k_mx)
 
         def weigh(b):
-            junk = keep.tile([NQ, N], F32, name="junk%d" % b)
-            shift = keep.tile([NQ, 1], F32, name="shift%d" % b)
-            nc.vector.tensor_scalar(junk[:], scores[b][:], -1.0, neg_sinks[b][:], ALU.mult, ALU.min, accum_out=shift[:])
-            prob = keep.tile([NQ, PACK, P], F32, name="prob%d" % b)
-            own = keep.tile([NQ, 1], F32, name="own%d" % b)
+            spare = keep.tile([NQ, N], F32, name="spare%d" % b)
+            shifts[b] = keep.tile([NQ, 1], F32, name="shift%d" % b)
+            nc.vector.tensor_scalar(spare[:], scores[b][:], -1.0, neg_sink[:, b : b + 1], ALU.mult, ALU.min, accum_out=shifts[b][:])
+            probs[b] = keep.tile([NQ, PACK, P], F32, name="prob%d" % b)
             nc.scalar.activation(
-                prob[:].rearrange("q t p -> q p t"),
+                probs[b][:].rearrange("q t p -> q p t"),
                 scores[b][:].rearrange("q (p t) -> q p t", t=PACK),
                 ACT.Exp,
-                bias=shift[:],
-                accum_out=own[:],
+                bias=shifts[b][:],
+                accum_out=own[:, b : b + 1],
             )
-            probs[b] = prob
-            shifts[b] = shift
-            sums[b] = own
-
-        for b in range(B):
-            v = keep.tile([P, NV, P, PACK], BF16, name="v_bf%d" % b, align_bytes=64)
-            v_bf[b] = v
 
         def turn_values(c, b):
             v_row = keep.tile([P, PACK, P], BF16, name="v_row%d%d" % (c, b))
             nc.vector.tensor_copy(v_row[:].rearrange("e t p -> e p t"), v_pool[c][:].indirect(listed(b)))
-            turned_v = banks.tile([P, PACK, P], BF16, name="turned_v", tag="turned_v", bufs=2)
+            turned = banks.tile([P, PACK, P], BF16, name="turned_v", tag="turned_v", bufs=2)
             for t in range(PACK):
-                nc.tensor.transpose(turned_v[:, t, :], v_row[:, t, :], ident_bf[:])
-            nc.scalar.copy(v_bf[b][:, c], turned_v[:].rearrange("p t e -> p e t"))
+                nc.tensor.transpose(turned[:, t, :], v_row[:, t, :], ident_bf[:])
+            v_bf[c, b] = keep.tile([P, P, PACK], BF16, name="v_bf%d%d" % (c, b), align_bytes=64)
+            nc.scalar.copy(v_bf[c, b][:], turned[:].rearrange("p t e -> p e t"))
 
-        score(0)
-        turn_values(0, 0)
-        score(1)
-        weigh(0)
-        turn_values(1, 0)
-        weigh(1)
-        turn_values(0, 1)
-        turn_values(1, 1)
-
-        sunk = []
-        for b in range(B):
-            s = keep.tile([NQ, 1], F32, name="sunk%d" % b)
-            nc.scalar.activation(s[:], sinks[b][:], ACT.Exp, bias=shifts[b][:])
-            sunk.append(s)
-
-        w_bf = []
-        for b in range(B):
+        def turn_weights(b):
             turned = banks.tile([P, PACK, P], F32, name="turned", tag="turned", bufs=2)
             for t in range(PACK):
                 nc.tensor.transpose(turned[:, t, :], probs[b][:, t, :], ident[:])
-            w = keep.tile([P, NQ, PACK], BF16, name="w_bf%d" % b, align_bytes=64)
+            w_bf[b] = keep.tile([P, NQ, PACK], BF16, name="w_bf%d" % b, align_bytes=64)
             nc.vector.tensor_tensor(
-                w[:],
+                w_bf[b][:],
                 turned[:].rearrange("p t q -> p q t"),
                 scale_col[:, b, :].unsqueeze(1).to_broadcast([P, NQ, PACK]),
                 ALU.mult,
             )
-            w_bf.append(w)
-        for b in range(B):
-            quantize(w_codes, b, w_bf[b][:].rearrange("p q t -> p (q t)"), NQ, "w")
-        for b in range(B):
-            quantize(v_codes, b, v_bf[b][:].rearrange("p c e t -> p (c e t)"), DV, "v")
 
-        inverses = []
+        def quantize_values(c, b):
+            v_mx[c, b] = quantize("v%d%d" % (c, b), v_bf[c, b][:].rearrange("p e t -> p (e t)"), P)
+
+        def quantize_weights(b):
+            w_mx[b] = quantize("w%d" % b, w_bf[b][:].rearrange("p q t -> p (q t)"), NQ)
+
+        q_mx = []
         for b in range(B):
-            total = keep.tile([NQ, 1], F32, name="total%d" % b)
-            nc.gpsimd.tensor_tensor(total[:], sums[b][:], sunk[b][:], ALU.add)
-            inverse = keep.tile([NQ, 1], F32, name="inverse%d" % b)
-            nc.vector.reciprocal(inverse[:], total[:])
-            inverses.append(inverse)
+            q_mx.append(quantize("q%d" % b, q_bf[:, b].rearrange("p q t -> p (q t)"), NQ))
+        score(0, q_mx[0])
+        turn_values(0, 0)
+        score(1, q_mx[1])
+        weigh(0)
+        turn_values(0, 1)
+        weigh(1)
+        turn_values(1, 0)
+        turn_values(1, 1)
+        sunk = keep.tile([NQ, B], F32, name="sunk", tag="spare1")
+        for b in range(B):
+            nc.scalar.activation(sunk[:, b : b + 1], sink_col[:, b : b + 1], ACT.Exp, bias=shifts[b][:])
+        total = keep.tile([NQ, B], F32, name="total")
+        nc.gpsimd.tensor_tensor(total[:], own[:], sunk[:], ALU.add)
+        quantize_values(0, 0)
+        turn_weights(0)
+        turn_weights(1)
+        quantize_weights(0)
+        quantize_values(0, 1)
+        quantize_weights(1)
+        inverse = keep.tile([NQ, B], F32, name="inverse")
+        nc.vector.reciprocal(inverse[:], total[:])
+        quantize_values(1, 0)
+        quantize_values(1, 1)
 
         for b in range(B):
             y = banks.tile([NQ, DV], F32, name="y", tag="y", bufs=2)
-            multiply(y[:], w_codes[b], v_codes[b])
+            for c in range(NV):
+                multiply(y[:, c * P : (c + 1) * P], w_mx[b], v_mx[c, b])
             result = keep.tile([NQ, DV], F32, name="result%d" % b)
-            nc.scalar.activation(result[:], y[:], ACT.Copy, scale=inverses[b][:])
+            nc.scalar.activation(result[:], y[:], ACT.Copy, scale=inverse[:, b : b + 1])
             nc.sync.dma_start(out[b], result[:])

@@ -38,7 +38,6 @@ def tile_attend_sink_kernel(tc, qT, kT, vT, vs, sink, offs, out):
         warm = keep.tile([P, 1], F32, name="warm")
         warmed = keep.tile([P, 1], F32, name="warmed")
         ident = keep.tile([P, P], F32, name="ident")
-        ident_bf = keep.tile([P, P], BF16, name="ident_bf")
 
         nc.sync.dma_start(offsets[:], offs)
         half = T // 2
@@ -69,7 +68,6 @@ def tile_attend_sink_kernel(tc, qT, kT, vT, vs, sink, offs, out):
             v_pool.append(w)
 
         make_identity(nc, ident[:])
-        make_identity(nc, ident_bf[:])
 
         turned_sink = banks.tile([P, PACK, P], F32, name="turned_sink", tag="turned", bufs=2)
         nc.tensor.transpose(turned_sink[:, 0, :], sink_rows[:], ident[:])
@@ -155,11 +153,11 @@ def tile_attend_sink_kernel(tc, qT, kT, vT, vs, sink, offs, out):
             )
 
         def turn_values(c, b):
-            v_row = keep.tile([P, PACK, P], BF16, name="v_row%d%d" % (c, b))
-            nc.vector.tensor_copy(v_row[:].rearrange("e t p -> e p t"), v_pool[c][:].indirect(listed(b)))
-            turned = banks.tile([P, PACK, P], BF16, name="turned_v", tag="turned_v", bufs=2)
+            v_row = keep.tile([P, N], F32, name="v_row%d%d" % (c, b))
+            nc.vector.tensor_copy(v_row[:], v_pool[c][:].indirect(listed(b)))
+            turned = banks.tile([P, PACK, P], F32, name="turned_v", tag="turned_v", bufs=2)
             for t in range(PACK):
-                nc.tensor.transpose(turned[:, t, :], v_row[:, t, :], ident_bf[:])
+                nc.tensor.transpose(turned[:, t, :], v_row[:, t::PACK], ident[:])
             v_bf[c, b] = keep.tile([P, P, PACK], BF16, name="v_bf%d%d" % (c, b), align_bytes=64)
             nc.scalar.copy(v_bf[c, b][:], turned[:].rearrange("p t e -> p e t"))
 

from contextlib import ExitStack

import concourse.mybir as mybir
from concourse.masks import make_identity

B, N, T, D, DV, NQ = 2, 512, 2048, 512, 256, 128
P = 128
PACK = 4
NV = DV // P

FLOPS = 2 * B * N * NQ * (D + DV)
BYTES = 4 * (B * D * NQ + D * T + DV * T + T + B * NQ + B * NQ * DV) + 2 * P * (B * N // 16)

F32 = mybir.dt.float32
BF16 = mybir.dt.bfloat16
U32 = mybir.dt.uint32
U16 = mybir.dt.uint16
U8 = mybir.dt.uint8
FP8X4 = mybir.dt.float8_e4m3fn_x4
ACT = mybir.ActivationFunctionType
ALU = mybir.AluOpType
AX = mybir.AxisListType


def tile_attend_sink_kernel(tc, qT, kT, vT, vs, sink, offs, out):
    nc = tc.nc
    with ExitStack() as ctx:
        keep = ctx.enter_context(tc.tile_pool(name="keep", bufs=1))
        banks = ctx.enter_context(tc.psum_pool(name="banks", bufs=1))

        offsets = keep.tile([P, B * N // 16], U16, name="offsets")

        def listed(b):
            return offsets[:, b * N // 16 : (b + 1) * N // 16]

        scale_pool = keep.tile([P, T], F32, name="scale_pool")
        sink_rows = keep.tile([P, P], F32, name="sink_rows")
        warm = keep.tile([P, 1], F32, name="warm")
        warmed = keep.tile([P, 1], F32, name="warmed")
        ident = keep.tile([P, P], F32, name="ident")

        nc.sync.dma_start(offsets[:], offs)
        half = T // 2
        nc.vector.memset(scale_pool[:, :half], 0.0)
        nc.gpsimd.memset(scale_pool[:, half:], 0.0)
        nc.gpsimd.memset(sink_rows[:], 0.0)
        nc.gpsimd.memset(warm[:], 0.0)
        nc.scalar.activation(warmed[:], warm[:], ACT.Exp)

        k_rows = kT.rearrange("(p t) c -> p t c", t=PACK)
        k_pool = []
        for t in range(PACK):
            w = keep.tile([P, T], F32, name="k_pool%d" % t)
            nc.sync.dma_start(w[:], k_rows[:, t, :])
            k_pool.append(w)
            if t == 0:
                nc.sync.dma_start(scale_pool[0:1, :], vs[0:1, :])
                nc.sync.dma_start(sink_rows[0:B, :], sink.rearrange("b q o -> b (q o)"))
        q_raw = []
        for b in range(B):
            q = keep.tile([P, PACK, NQ], F32, name="q_raw%d" % b)
            nc.sync.dma_start(q[:], qT[b].rearrange("(p t) q -> p t q", t=PACK))
            q_raw.append(q)
        v_pool = []
        for c in range(NV):
            w = keep.tile([P, T], F32, name="v_pool%d" % c)
            nc.sync.dma_start(w[:], vT[c * P : (c + 1) * P, :])
            v_pool.append(w)

        make_identity(nc, ident[:])

        turned_sink = banks.tile([P, PACK, P], F32, name="turned_sink", tag="turned", bufs=2)
        nc.tensor.transpose(turned_sink[:, 0, :], sink_rows[:], ident[:])
        sink_col = keep.tile([NQ, B], F32, name="sink_col")
        nc.scalar.copy(sink_col[:], turned_sink[:, 0, 0:B])
        neg_sink = keep.tile([NQ, B], F32, name="neg_sink")
        nc.gpsimd.tensor_scalar(neg_sink[:], sink_col[:], -1.0, None, ALU.mult)

        k_bf = []
        for b in range(B):
            k = keep.tile([P, N, PACK], BF16, name="k_bf%d" % b, align_bytes=64)
            k_bf.append(k)
        k_low = keep.tile([P, 2, B * N], F32, name="k_low", tag="low", align_bytes=64)
        k_high = keep.tile([P, 2, B * N], F32, name="k_high")

        def pair(copy, b, planes, t0):
            copy(k_bf[b][:, :, t0 : t0 + 2], planes[:, :, b * N : (b + 1) * N].rearrange("p t n -> p n t"))

        nc.vector.tensor_copy(k_low[:, 0, :], k_pool[0][:].indirect(offsets[:]))
        scale_row = keep.tile([P, B * N], F32, name="scale_row")
        nc.vector.tensor_copy(scale_row[:], scale_pool[:].indirect(offsets[:]))
        scale_col = keep.tile([P, B, PACK], F32, name="scale_col")
        for b in range(B):
            turned = banks.tile([P, PACK, P], F32, name="turned", tag="turned", bufs=2)
            for t in range(PACK):
                nc.tensor.transpose(turned[:, t, :], scale_row[:, b * N + t : (b + 1) * N : PACK], ident[:])
            nc.scalar.copy(scale_col[:, b, :], turned[:, :, 0])
        nc.vector.tensor_copy(k_low[:, 1, :], k_pool[1][:].indirect(offsets[:]))
        nc.vector.tensor_copy(k_high[:, 0, :], k_pool[2][:].indirect(offsets[:]))
        pair(nc.scalar.copy, 0, k_low, 0)
        pair(nc.vector.tensor_copy, 1, k_low, 0)
        for b in range(B):
            nc.vector.tensor_copy(k_high[:, 1, b * N : (b + 1) * N], k_pool[3][:].indirect(listed(b)))
        pair(nc.vector.tensor_copy, 0, k_high, 2)
        pair(nc.scalar.copy, 1, k_high, 2)

        q_bf = keep.tile([P, B, NQ, PACK], BF16, name="q_bf", tag="low", align_bytes=64)
        for b in range(B):
            nc.scalar.copy(q_bf[:, b], q_raw[b][:].rearrange("p t q -> p q t"))

        def quantize(name, source, width):
            codes = keep.tile([P, width], U32, name=name + "_codes", align_bytes=64)
            scales = keep.tile([P, width], U8, name=name + "_scales", align_bytes=64)
            nc.vector.quantize_mx(codes[:].bitcast(FP8X4), scales[:], source)
            return codes, scales

        def multiply(bank, left, right):
            nc.tensor.matmul_mx(
                out=bank,
                lhsT=left[0][:].bitcast(FP8X4),
                lhsT_scale=left[1][:],
                rhs=right[0][:].bitcast(FP8X4),
                rhs_scale=right[1][:],
                start=True,
                stop=True,
            )

        scores = {}
        probs = {}
        shifts = {}
        v_bf = {}
        w_bf = {}
        w_mx = {}
        v_mx = {}
        own = keep.tile([NQ, B], F32, name="own")

        def score(b, q_mx):
            k_mx = quantize("k%d" % b, k_bf[b][:].rearrange("p n t -> p (n t)"), N)
            scores[b] = banks.tile([NQ, N], F32, name="score", tag="score", bufs=2)
            multiply(scores[b][:], q_mx, k_mx)

        def weigh(b):
            spare = keep.tile([NQ, N], F32, name="spare%d" % b)
            shifts[b] = keep.tile([NQ, 1], F32, name="shift%d" % b)
            nc.vector.tensor_scalar(spare[:], scores[b][:], -1.0, neg_sink[:, b : b + 1], ALU.mult, ALU.min, accum_out=shifts[b][:])
            probs[b] = keep.tile([NQ, PACK, P], F32, name="prob%d" % b)
            nc.scalar.activation(
                probs[b][:].rearrange("q t p -> q p t"),
                scores[b][:].rearrange("q (p t) -> q p t", t=PACK),
                ACT.Exp,
                bias=shifts[b][:],
                accum_out=own[:, b : b + 1],
            )

        def turn_values(c, b):
            v_row = keep.tile([P, N], F32, name="v_row%d%d" % (c, b))
            nc.vector.tensor_copy(v_row[:], v_pool[c][:].indirect(listed(b)))
            turned = banks.tile([P, PACK, P], F32, name="turned_v", tag="turned_v", bufs=2)
            for t in range(PACK):
                nc.tensor.transpose(turned[:, t, :], v_row[:, t::PACK], ident[:])
            v_bf[c, b] = keep.tile([P, P, PACK], BF16, name="v_bf%d%d" % (c, b), align_bytes=64)
            nc.scalar.copy(v_bf[c, b][:], turned[:].rearrange("p t e -> p e t"))

        def turn_weights(b):
            turned = banks.tile([P, PACK, P], F32, name="turned", tag="turned", bufs=2)
            for t in range(PACK):
                nc.tensor.transpose(turned[:, t, :], probs[b][:, t, :], ident[:])
            w_bf[b] = keep.tile([P, NQ, PACK], BF16, name="w_bf%d" % b, align_bytes=64)
            nc.vector.tensor_tensor(
                w_bf[b][:],
                turned[:].rearrange("p t q -> p q t"),
                scale_col[:, b, :].unsqueeze(1).to_broadcast([P, NQ, PACK]),
                ALU.mult,
            )

        def quantize_values(c, b):
            v_mx[c, b] = quantize("v%d%d" % (c, b), v_bf[c, b][:].rearrange("p e t -> p (e t)"), P)

        def quantize_weights(b):
            w_mx[b] = quantize("w%d" % b, w_bf[b][:].rearrange("p q t -> p (q t)"), NQ)

        q_mx = []
        for b in range(B):
            q_mx.append(quantize("q%d" % b, q_bf[:, b].rearrange("p q t -> p (q t)"), NQ))
        score(0, q_mx[0])
        turn_values(0, 0)
        score(1, q_mx[1])
        weigh(0)
        turn_values(0, 1)
        weigh(1)
        turn_values(1, 0)
        turn_values(1, 1)
        sunk = keep.tile([NQ, B], F32, name="sunk", tag="spare1")
        for b in range(B):
            nc.scalar.activation(sunk[:, b : b + 1], sink_col[:, b : b + 1], ACT.Exp, bias=shifts[b][:])
        total = keep.tile([NQ, B], F32, name="total")
        nc.gpsimd.tensor_tensor(total[:], own[:], sunk[:], ALU.add)
        quantize_values(0, 0)
        turn_weights(0)
        turn_weights(1)
        quantize_weights(0)
        quantize_values(0, 1)
        quantize_weights(1)
        inverse = keep.tile([NQ, B], F32, name="inverse")
        nc.vector.reciprocal(inverse[:], total[:])
        quantize_values(1, 0)
        quantize_values(1, 1)

        for b in range(B):
            y = banks.tile([NQ, DV], F32, name="y", tag="y", bufs=2)
            for c in range(NV):
                multiply(y[:, c * P : (c + 1) * P], w_mx[b], v_mx[c, b])
            result = keep.tile([NQ, DV], F32, name="result%d" % b)
            nc.scalar.activation(result[:], y[:], ACT.Copy, scale=inverse[:, b : b + 1])
            nc.sync.dma_start(out[b], result[:])
